import numpy as np
import ml_dtypes


def mxq(x, axis, fmt="e4m3"):
    dtype, down = {"e4m3": (ml_dtypes.float8_e4m3fn, 7), "e5m2": (ml_dtypes.float8_e5m2, 14)}[fmt]
    v = np.moveaxis(np.asarray(x, np.float32).astype(ml_dtypes.bfloat16).astype(np.float64), axis, -1)
    blocks = v.reshape(v.shape[:-1] + (-1, 32))
    amax = np.abs(blocks).max(-1, keepdims=True)
    byte = np.maximum(np.where(amax > 0, np.frexp(amax)[1] - 1 + 127, 0) - down, 1)
    scale = np.exp2(byte - 127.0)
    codes = (blocks / scale).astype(np.float32).astype(dtype).astype(np.float64)
    return np.moveaxis((codes * scale).reshape(v.shape), -1, axis)


WIDE = False


def mx_kscale(k):
    if not WIDE:
        return np.ones(k)
    levels = np.array([10, -10, 5, -5, 0])
    if k % 512:
        return np.exp2(np.random.permutation(np.resize(levels, k // 32))).repeat(32)
    a = np.empty((k // 512, 16))
    for p in range(k // 512):
        a[p, :8] = np.random.permutation(np.resize(levels, 8))
        for g in range(8):
            far = levels[np.abs(levels - a[p, g]) >= 10]
            a[p, g + 8] = far[np.random.randint(len(far))]
    return np.exp2(a.ravel()).repeat(32)


def f64(x):
    return np.asarray(x).astype(np.float64)


def striped(idx):
    return np.tile(np.asarray(idx).reshape(-1, 16).T, (8, 1)).astype(np.uint16)


def unstriped(offs):
    return offs[:16].T.reshape(-1).astype(np.int64)


E2M1 = np.array([0.0, 0.5, 1.0, 1.5, 2.0, 3.0, 4.0, 6.0, -0.0, -0.5, -1.0, -1.5, -2.0, -3.0, -4.0, -6.0])


def pack_weight(w, fmt):
    k, n = w.shape
    w = f64(np.asarray(w, np.float32).astype(ml_dtypes.bfloat16)).reshape(k // 32, 32, n)
    amax = np.abs(w).max(1)
    if fmt == "e4m3":
        byte = np.frexp(amax)[1] - 1 + 127 - 7
    else:
        mant, ex = np.frexp(amax / 6.0)
        byte = np.where(mant > 0.5, ex, ex - 1) + 127
    byte = np.clip(np.where(amax > 0, byte, 1), 1, 254)
    scaled = (w * np.exp2(127.0 - byte)[:, None, :]).reshape(k, n).astype(np.float32)
    by_word = np.ascontiguousarray(scaled.reshape(k // 512, 128, 4, n).transpose(0, 1, 3, 2))
    if fmt == "e4m3":
        words = by_word.astype(ml_dtypes.float8_e4m3fn).view(np.uint8)
    else:
        c = by_word.astype(ml_dtypes.float4_e2m1fn).view(np.uint8) & 0xF
        words = (c[..., 0::2] | (c[..., 1::2] << 4)).reshape(k // 512, 128, 2 * n)
    return np.ascontiguousarray(words), np.ascontiguousarray(byte.astype(np.uint8).reshape(k // 512, 16, n))


def unpack_weight(words, scales, fmt):
    g, _, n = scales.shape
    words = np.ascontiguousarray(words).reshape(g, 128, n, -1)
    if fmt == "e4m3":
        vals = words.view(ml_dtypes.float8_e4m3fn).astype(np.float64)
    else:
        nib = np.empty((g, 128, n, 4), np.uint8)
        nib[..., 0::2] = words & 0xF
        nib[..., 1::2] = words >> 4
        vals = E2M1[nib]
    vals = vals * np.repeat(np.exp2(scales.astype(np.float64) - 127.0), 8, axis=1)[..., None]
    return vals.transpose(0, 1, 3, 2).reshape(g * 512, n)


def softplus(v):
    return np.log(1.0 + np.exp(v))


K, T, J, L, N = 512, 2048, 512, 512, 512


def setup_inputs():
    n = np.random.standard_normal
    idx = np.random.permutation(T)[:J]
    fk = mx_kscale(K)
    fl = mx_kscale(L)
    xtp = pack_weight(n((K, T)) / fk[:, None], "e4m3")
    wap = pack_weight(n((K, N)) * 1 / np.sqrt(K) * fk[:, None], "e2m1")
    vap = pack_weight(n((K, N)) * 1 / np.sqrt(K) * fk[:, None], "e4m3")
    sxp = pack_weight(n((L, J)) / fl[:, None], "e2m1")
    vbp = pack_weight(n((L, N)) * 1 / np.sqrt(L) * fl[:, None], "e4m3")
    return {
        "xt_words": xtp[0],
        "xt_scales": xtp[1],
        "wa_words": wap[0],
        "wa_scales": wap[1],
        "va_words": vap[0],
        "va_scales": vap[1],
        "sx_words": sxp[0],
        "sx_scales": sxp[1],
        "wb": (n((L, N)) * 1 / np.sqrt(L) * fl[:, None]).astype(np.float32),
        "vb_words": vbp[0],
        "vb_scales": vbp[1],
        "offs": striped(idx),
    }


def reference(xt_words, xt_scales, wa_words, wa_scales, va_words, va_scales, sx_words, sx_scales, wb, vb_words, vb_scales, offs):
    idx = unstriped(offs)
    xtu = unpack_weight(xt_words, xt_scales, "e4m3")
    wau = unpack_weight(wa_words, wa_scales, "e2m1")
    vau = unpack_weight(va_words, va_scales, "e4m3")
    sxu = unpack_weight(sx_words, sx_scales, "e2m1")
    vbu = unpack_weight(vb_words, vb_scales, "e4m3")
    xtidxg = xtu[:, idx]
    a = wau.T @ xtidxg
    u = vau.T @ xtidxg
    wbq = mxq(f64(wb), 0, "e4m3")
    b = wbq.T @ sxu
    v = vbu.T @ sxu
    pa = softplus(u)
    pb = softplus(v)
    y = (pa * a + pb * b) / (pa + pb + 0.1)
    return y

@@ -1,0 +1,193 @@
+from contextlib import ExitStack
+
+import concourse.mybir as mybir
+
+K, T, J, L, N = 512, 2048, 512, 512, 512
+FLOPS = 4 * 2 * 512 * 512 * 512
+
+F32 = mybir.dt.float32
+BF16 = mybir.dt.bfloat16
+I32 = mybir.dt.int32
+U32 = mybir.dt.uint32
+U16 = mybir.dt.uint16
+U8 = mybir.dt.uint8
+FP8X4 = mybir.dt.float8_e4m3fn_x4
+FP4X4 = mybir.dt.float4_e2m1fn_x4
+ACT = mybir.ActivationFunctionType
+ALU = mybir.AluOpType
+
+P = 128
+HALF = J // 2
+PIECES = 4
+WIDTH = 512
+EXP_CAP = float(2 ** 62)
+
+
+def load_scale_rows(queue, plane, scales, quads):
+    for quad in quads:
+        queue.dma_start(
+            out=plane[32 * quad : 32 * quad + 4, :].bitcast(I32),
+            in_=scales[0, 4 * quad : 4 * quad + 4, :].bitcast(I32),
+        )
+
+
+def fp8_words(words):
+    return words[0].rearrange("p n t -> p (n t)").bitcast(I32)
+
+
+def tile_list_precision_weighted_pair_kernel(
+    tc, xt_words, xt_scales, wa_words, wa_scales, va_words, va_scales,
+    sx_words, sx_scales, wb, vb_words, vb_scales, offs, out,
+):
+    nc = tc.nc
+    with ExitStack() as ctx:
+        keep = ctx.enter_context(tc.tile_pool(name="keep", bufs=1))
+        shared = ctx.enter_context(tc.tile_pool(name="shared", bufs=1))
+        psum = ctx.enter_context(tc.psum_pool(name="psum", bufs=1))
+
+        offsets = keep.tile([P, J // 16], U16, name="offsets")
+        xt_w = keep.tile([P, T], U32, name="xt_w", align_bytes=64)
+        xt_s = keep.tile([P, T], U8, name="xt_s", align_bytes=64)
+        sx_w = keep.tile([P, 2 * J], U8, name="sx_w", align_bytes=64)
+        vb_w = keep.tile([P, N], U32, name="vb_w", align_bytes=64)
+        staged = shared.tile([16, 3, N], U8, name="staged", align_bytes=64, offset=7936)
+        planes = keep.tile([P, 3, N], U8, name="planes", align_bytes=64)
+        sx_s, vb_s, va_s = planes[:, 0, :], planes[:, 1, :], planes[:, 2, :]
+        wa_s = keep.tile([P, N], U8, name="wa_s", align_bytes=64)
+        wb_bf = keep.tile([P, N, 4], BF16, name="wb_bf", align_bytes=64)
+        wb_w = keep.tile([P, N], U32, name="wb_w", align_bytes=64)
+        wb_s = keep.tile([P, N], U8, name="wb_s", align_bytes=64)
+        xg_w = [keep.tile([P, HALF], U32, name="xg_w%d" % h, align_bytes=64) for h in range(2)]
+        xg_s = keep.tile([P, J], U8, name="xg_s", align_bytes=64)
+
+        nc.gpsimd.memset(xt_s[:].bitcast(I32), 0)
+        nc.vector.memset(planes[:].rearrange("p a n -> p (a n)").bitcast(I32), 0)
+        nc.vector.memset(wa_s[:].bitcast(I32), 0)
+
+        for place, scales in enumerate((sx_scales, vb_scales, va_scales)):
+            nc.sync.dma_start(out=staged[:, place, :].bitcast(I32), in_=scales[0].bitcast(I32))
+        nc.sync.dma_start(offsets[:], offs)
+        nc.sync.dma_start(out=sx_w[:].bitcast(I32), in_=sx_words[0].bitcast(I32))
+        nc.sync.dma_start(out=vb_w[:].bitcast(I32), in_=fp8_words(vb_words))
+        load_scale_rows(nc.sync, xt_s, xt_scales, (0,))
+        nc.sync.dma_start(out=xt_w[:].bitcast(I32), in_=fp8_words(xt_words))
+        load_scale_rows(nc.sync, xt_s, xt_scales, (1,))
+        load_scale_rows(nc.gpsimd, xt_s, xt_scales, (2, 3))
+        for quad in range(4):
+            nc.sync.dma_start(
+                out=planes[32 * quad : 32 * quad + 4].rearrange("p a n -> p (a n)").bitcast(I32),
+                in_=staged[4 * quad : 4 * quad + 4].rearrange("p a n -> p (a n)").bitcast(I32),
+            )
+        wb_raw = shared.tile([P, 2, 4, N // 2], F32, name="wb_raw", align_bytes=64, offset=0)
+        wa_w = shared.tile([P, 2 * N], U8, name="wa_w", align_bytes=64, offset=8192)
+        va_w = shared.tile([P, N], U32, name="va_w", align_bytes=64, offset=9216)
+        nc.sync.dma_start(out=va_w[:].bitcast(I32), in_=fp8_words(va_words))
+        for half in range(2):
+            nc.sync.dma_start(
+                out=wb_raw[:, half],
+                in_=wb[:, half * (N // 2) : (half + 1) * (N // 2)].rearrange("(p t) n -> p t n", t=4),
+            )
+        nc.sync.dma_start(out=wa_w[:].bitcast(I32), in_=wa_words[0].bitcast(I32))
+        load_scale_rows(nc.gpsimd, wa_s, wa_scales, range(4))
+
+        def product(bank, q, weights, weight_scales, moving, moving_scales):
+            h, pair = divmod(q, 2)
+            acc = psum.tile([P, WIDTH], F32, name="acc", tag="bank%d" % bank)
+            for s in range(2):
+                nt = 2 * pair + s
+                nc.tensor.matmul_mx(
+                    out=acc[:, s * HALF : (s + 1) * HALF],
+                    lhsT=weights(nt),
+                    lhsT_scale=weight_scales[:, nt * P : (nt + 1) * P],
+                    rhs=moving(h),
+                    rhs_scale=moving_scales[:, h * HALF : (h + 1) * HALF],
+                    start=True,
+                    stop=True,
+                )
+            return acc
+
+        def fp8_columns(words):
+            return lambda nt: words[:, nt * P : (nt + 1) * P].bitcast(FP8X4)
+
+        def wa_columns(nt):
+            return wa_w[:, 2 * nt * P : 2 * (nt + 1) * P].bitcast(FP4X4)
+
+        def sx_half(h):
+            return sx_w[:, 2 * h * HALF : 2 * (h + 1) * HALF].bitcast(FP4X4)
+
+        def xg_half(h):
+            return xg_w[h][:].bitcast(FP8X4)
+
+        grown = keep.tile([P, PIECES, 2, WIDTH], F32, name="grown")
+        logs = keep.tile([P, PIECES, 2, WIDTH], F32, name="logs")
+        prec = keep.tile([P, PIECES, 2, WIDTH], F32, name="prec")
+        terms = keep.tile([P, PIECES, 2, WIDTH], F32, name="terms")
+        den = keep.tile([P, PIECES, WIDTH], F32, name="den")
+        log_den = keep.tile([P, PIECES, WIDTH], F32, name="log_den")
+        num = keep.tile([P, PIECES, WIDTH], F32, name="num")
+        result = keep.tile([P, PIECES, WIDTH], F32, name="result")
+
+        def grow(q, side, acc):
+            nc.scalar.activation(out=grown[:, q, side, :], in_=acc[:], func=ACT.Exp)
+            nc.vector.tensor_scalar(
+                out=grown[:, q, side, :], in0=grown[:, q, side, :],
+                scalar1=EXP_CAP, scalar2=None, op0=ALU.min,
+            )
+
+        v = [product(q, q, fp8_columns(vb_w), vb_s, sx_half, sx_s) for q in range(PIECES)]
+        for h in range(2):
+            listed = offsets[:, h * (HALF // 16) : (h + 1) * (HALF // 16)]
+            nc.vector.tensor_copy(xg_s[:, h * HALF : (h + 1) * HALF], xt_s[:].indirect(listed))
+            nc.vector.tensor_copy(xg_w[h][:], xt_w[:].indirect(listed))
+        u = [product(PIECES + q, q, fp8_columns(va_w), va_s, xg_half, xg_s) for q in range(PIECES)]
+        for q in range(PIECES):
+            grow(q, 1, v[q])
+        for q in range(PIECES):
+            grow(q, 0, u[q])
+
+        for half in range(2):
+            cols = slice(half * (N // 2), (half + 1) * (N // 2))
+            nc.vector.tensor_copy(
+                out=wb_bf[:, cols, :].rearrange("p (c i) t -> p c t i", i=4),
+                in_=wb_raw[:, half].rearrange("p t (c i) -> p c t i", i=4),
+            )
+        for half in range(2):
+            cols = slice(half * (N // 2), (half + 1) * (N // 2))
+            nc.vector.quantize_mx(
+                out=wb_w[:, cols].bitcast(FP8X4),
+                scales=wb_s[:, cols],
+                in_=wb_bf[:, cols, :].rearrange("p n t -> p (n t)"),
+            )
+
+        for q in range(PIECES):
+            nc.scalar.activation(out=logs[:, q], in_=grown[:, q], func=ACT.Ln, bias=1.0)
+        for q in range(PIECES):
+            nc.vector.tensor_tensor(out=prec[:, q, 0, :], in0=u[q][:], in1=logs[:, q, 0, :], op=ALU.max)
+            nc.vector.tensor_tensor(out=prec[:, q, 1, :], in0=v[q][:], in1=logs[:, q, 1, :], op=ALU.max)
+            nc.gpsimd.tensor_tensor(out=den[:, q, :], in0=prec[:, q, 0, :], in1=prec[:, q, 1, :], op=ALU.add)
+        for q in range(PIECES):
+            nc.scalar.activation(out=log_den[:, q, :], in_=den[:, q, :], func=ACT.Ln, bias=0.1)
+        for q in range(PIECES):
+            a = product(PIECES + q, q, wa_columns, wa_s, xg_half, xg_s)
+            b = product(q, q, fp8_columns(wb_w), wb_s, sx_half, sx_s)
+            nc.vector.tensor_tensor(out=terms[:, q, 0, :], in0=a[:], in1=prec[:, q, 0, :], op=ALU.mult)
+            nc.vector.tensor_tensor(out=terms[:, q, 1, :], in0=b[:], in1=prec[:, q, 1, :], op=ALU.mult)
+            adder = nc.vector if q == PIECES - 1 else nc.gpsimd
+            adder.tensor_tensor(out=num[:, q, :], in0=terms[:, q, 0, :], in1=terms[:, q, 1, :], op=ALU.add)
+
+        for q in range(PIECES):
+            h, pair = divmod(q, 2)
+            inverse = den[:, :, q * P : (q + 1) * P]
+            nc.scalar.activation(
+                out=inverse, in_=log_den[:, q, :].rearrange("p (a c) -> p a c", c=P), func=ACT.Exp, scale=-1.0
+            )
+            nc.vector.tensor_tensor(
+                out=result[:, q, :].rearrange("p (a c) -> p a c", c=P),
+                in0=num[:, q, :].rearrange("p (a c) -> p a c", c=P),
+                in1=inverse,
+                op=ALU.mult,
+            )
+            nc.sync.dma_start(
+                out=out[2 * pair * P : 2 * (pair + 1) * P, h * HALF : (h + 1) * HALF].rearrange("(s p) j -> p s j", p=P),
+                in_=result[:, q, :].rearrange("p (s j) -> p s j", s=2),
+            )

@@ -60,23 +60,23 @@ def tile_list_precision_weighted_pair_kernel(
         xg_w = [keep.tile([P, HALF], U32, name="xg_w%d" % h, align_bytes=64) for h in range(2)]
         xg_s = keep.tile([P, J], U8, name="xg_s", align_bytes=64)
 
-        nc.gpsimd.memset(xt_s[:].bitcast(I32), 0)
+        nc.vector.memset(xt_s[:].bitcast(I32), 0)
         nc.vector.memset(planes[:].rearrange("p a n -> p (a n)").bitcast(I32), 0)
-        nc.vector.memset(wa_s[:].bitcast(I32), 0)
+        nc.gpsimd.memset(wa_s[:].bitcast(I32), 0)
 
         for place, scales in enumerate((sx_scales, vb_scales, va_scales)):
             nc.sync.dma_start(out=staged[:, place, :].bitcast(I32), in_=scales[0].bitcast(I32))
+        nc.scalar.dma_start(out=sx_w[:].bitcast(I32), in_=sx_words[0].bitcast(I32))
+        nc.scalar.dma_start(out=vb_w[:].bitcast(I32), in_=fp8_words(vb_words))
         nc.sync.dma_start(offsets[:], offs)
-        nc.sync.dma_start(out=sx_w[:].bitcast(I32), in_=sx_words[0].bitcast(I32))
-        nc.sync.dma_start(out=vb_w[:].bitcast(I32), in_=fp8_words(vb_words))
-        load_scale_rows(nc.sync, xt_s, xt_scales, (0,))
         nc.sync.dma_start(out=xt_w[:].bitcast(I32), in_=fp8_words(xt_words))
-        load_scale_rows(nc.sync, xt_s, xt_scales, (1,))
-        load_scale_rows(nc.gpsimd, xt_s, xt_scales, (2, 3))
-        for quad in range(4):
+        load_scale_rows(nc.sync, xt_s, xt_scales, range(4))
+        staged_words = staged[:].rearrange("p a n -> p (a n)").bitcast(I32)
+        plane_words = planes[:].rearrange("p a n -> p (a n)").bitcast(I32)
+        nc.vector.tensor_copy(out=plane_words[0:4], in_=staged_words[0:4])
+        for quad in range(1, 4):
             nc.sync.dma_start(
-                out=planes[32 * quad : 32 * quad + 4].rearrange("p a n -> p (a n)").bitcast(I32),
-                in_=staged[4 * quad : 4 * quad + 4].rearrange("p a n -> p (a n)").bitcast(I32),
+                out=plane_words[32 * quad : 32 * quad + 4], in_=staged_words[4 * quad : 4 * quad + 4]
             )
         wb_raw = shared.tile([P, 2, 4, N // 2], F32, name="wb_raw", align_bytes=64, offset=0)
         wa_w = shared.tile([P, 2 * N], U8, name="wa_w", align_bytes=64, offset=8192)
@@ -118,21 +118,25 @@ def tile_list_precision_weighted_pair_kernel(
         def xg_half(h):
             return xg_w[h][:].bitcast(FP8X4)
 
-        grown = keep.tile([P, PIECES, 2, WIDTH], F32, name="grown")
-        logs = keep.tile([P, PIECES, 2, WIDTH], F32, name="logs")
+        exp_u = keep.tile([P, PIECES, WIDTH], F32, name="exp_u")
+        capped_u = keep.tile([P, PIECES, WIDTH], F32, name="capped_u")
+        capped_v = keep.tile([P, PIECES, WIDTH], F32, name="capped_v")
         prec = keep.tile([P, PIECES, 2, WIDTH], F32, name="prec")
-        terms = keep.tile([P, PIECES, 2, WIDTH], F32, name="terms")
+        late_terms = keep.tile([P, 2, 2, WIDTH], F32, name="late_terms")
         den = keep.tile([P, PIECES, WIDTH], F32, name="den")
         log_den = keep.tile([P, PIECES, WIDTH], F32, name="log_den")
         num = keep.tile([P, PIECES, WIDTH], F32, name="num")
         result = keep.tile([P, PIECES, WIDTH], F32, name="result")
 
-        def grow(q, side, acc):
-            nc.scalar.activation(out=grown[:, q, side, :], in_=acc[:], func=ACT.Exp)
-            nc.vector.tensor_scalar(
-                out=grown[:, q, side, :], in0=grown[:, q, side, :],
-                scalar1=EXP_CAP, scalar2=None, op0=ALU.min,
-            )
+        def quarters(ap):
+            return ap.rearrange("p (a c) -> p a c", c=P)
+
+        def across(tile, q):
+            return tile[:, :, q * P : (q + 1) * P]
+
+        def capped_exp(acc, grown, capped):
+            nc.scalar.activation(out=grown, in_=acc[:], func=ACT.Exp)
+            nc.vector.tensor_scalar(out=capped, in0=grown, scalar1=EXP_CAP, scalar2=None, op0=ALU.min)
 
         v = [product(q, q, fp8_columns(vb_w), vb_s, sx_half, sx_s) for q in range(PIECES)]
         for h in range(2):
@@ -141,9 +145,9 @@ def tile_list_precision_weighted_pair_kernel(
             nc.vector.tensor_copy(xg_w[h][:], xt_w[:].indirect(listed))
         u = [product(PIECES + q, q, fp8_columns(va_w), va_s, xg_half, xg_s) for q in range(PIECES)]
         for q in range(PIECES):
-            grow(q, 1, v[q])
+            capped_exp(v[q], capped_v[:, q, :], capped_v[:, q, :])
         for q in range(PIECES):
-            grow(q, 0, u[q])
+            capped_exp(u[q], exp_u[:, q, :], capped_u[:, q, :])
 
         for half in range(2):
             cols = slice(half * (N // 2), (half + 1) * (N // 2))
@@ -160,34 +164,49 @@ def tile_list_precision_weighted_pair_kernel(
             )
 
         for q in range(PIECES):
-            nc.scalar.activation(out=logs[:, q], in_=grown[:, q], func=ACT.Ln, bias=1.0)
+            nc.scalar.activation(out=across(exp_u, q), in_=quarters(capped_v[:, q, :]), func=ACT.Ln, bias=1.0)
+            nc.scalar.activation(out=capped_v[:, q, :], in_=capped_u[:, q, :], func=ACT.Ln, bias=1.0)
         for q in range(PIECES):
-            nc.vector.tensor_tensor(out=prec[:, q, 0, :], in0=u[q][:], in1=logs[:, q, 0, :], op=ALU.max)
-            nc.vector.tensor_tensor(out=prec[:, q, 1, :], in0=v[q][:], in1=logs[:, q, 1, :], op=ALU.max)
+            nc.vector.tensor_tensor(
+                out=quarters(prec[:, q, 1, :]), in0=quarters(v[q][:]), in1=across(exp_u, q), op=ALU.max
+            )
+            nc.vector.tensor_tensor(out=prec[:, q, 0, :], in0=u[q][:], in1=capped_v[:, q, :], op=ALU.max)
             nc.gpsimd.tensor_tensor(out=den[:, q, :], in0=prec[:, q, 0, :], in1=prec[:, q, 1, :], op=ALU.add)
         for q in range(PIECES):
             nc.scalar.activation(out=log_den[:, q, :], in_=den[:, q, :], func=ACT.Ln, bias=0.1)
-        for q in range(PIECES):
-            a = product(PIECES + q, q, wa_columns, wa_s, xg_half, xg_s)
-            b = product(q, q, fp8_columns(wb_w), wb_s, sx_half, sx_s)
-            nc.vector.tensor_tensor(out=terms[:, q, 0, :], in0=a[:], in1=prec[:, q, 0, :], op=ALU.mult)
-            nc.vector.tensor_tensor(out=terms[:, q, 1, :], in0=b[:], in1=prec[:, q, 1, :], op=ALU.mult)
-            adder = nc.vector if q == PIECES - 1 else nc.gpsimd
-            adder.tensor_tensor(out=num[:, q, :], in0=terms[:, q, 0, :], in1=terms[:, q, 1, :], op=ALU.add)
+
+        def term(q, side):
+            return across(capped_v, 2 * q + side) if q < 2 else quarters(late_terms[:, q - 2, side, :])
+
+        def add_terms(engine, q):
+            engine.tensor_tensor(out=quarters(num[:, q, :]), in0=term(q, 0), in1=term(q, 1), op=ALU.add)
 
         for q in range(PIECES):
+            b = product(q, q, fp8_columns(wb_w), wb_s, sx_half, sx_s)
+            a = product(PIECES + q, q, wa_columns, wa_s, xg_half, xg_s)
+            nc.vector.tensor_tensor(out=term(q, 1), in0=quarters(b[:]), in1=quarters(prec[:, q, 1, :]), op=ALU.mult)
+            nc.vector.tensor_tensor(out=term(q, 0), in0=quarters(a[:]), in1=quarters(prec[:, q, 0, :]), op=ALU.mult)
+            if q < 2:
+                add_terms(nc.gpsimd, q)
+        for q in range(2, PIECES):
+            add_terms(nc.vector, q)
+
+        for q in range(PIECES):
+            nc.scalar.activation(out=across(den, q), in_=quarters(log_den[:, q, :]), func=ACT.Exp, scale=-1.0)
+        for q in range(PIECES):
             h, pair = divmod(q, 2)
-            inverse = den[:, :, q * P : (q + 1) * P]
-            nc.scalar.activation(
-                out=inverse, in_=log_den[:, q, :].rearrange("p (a c) -> p a c", c=P), func=ACT.Exp, scale=-1.0
-            )
-            nc.vector.tensor_tensor(
-                out=result[:, q, :].rearrange("p (a c) -> p a c", c=P),
-                in0=num[:, q, :].rearrange("p (a c) -> p a c", c=P),
-                in1=inverse,
-                op=ALU.mult,
-            )
-            nc.sync.dma_start(
-                out=out[2 * pair * P : 2 * (pair + 1) * P, h * HALF : (h + 1) * HALF].rearrange("(s p) j -> p s j", p=P),
-                in_=result[:, q, :].rearrange("p (s j) -> p s j", s=2),
-            )
+            steps = 2 if q == PIECES - 1 else 1
+            for step in range(steps):
+                part = slice(step * 4 // steps, (step + 1) * 4 // steps)
+                tiles = slice(step * 2 // steps, (step + 1) * 2 // steps)
+                nc.vector.tensor_tensor(
+                    out=quarters(result[:, q, :])[:, part],
+                    in0=quarters(num[:, q, :])[:, part],
+                    in1=across(den, q)[:, part],
+                    op=ALU.mult,
+                )
+                rows = out[2 * pair * P : 2 * (pair + 1) * P, h * HALF : (h + 1) * HALF]
+                nc.sync.dma_start(
+                    out=rows.rearrange("(s p) j -> p s j", p=P)[:, tiles],
+                    in_=result[:, q, :].rearrange("p (s j) -> p s j", s=2)[:, tiles],
+                )

@@ -1,9 +1,10 @@
 from contextlib import ExitStack
 
 import concourse.mybir as mybir
+from concourse.masks import make_identity
 
-K, T, J, L, N = 512, 2048, 512, 512, 512
-FLOPS = 4 * 2 * 512 * 512 * 512
+K, T, J, N = 512, 2048, 512, 512
+FLOPS = 4 * 2 * K * J * N
 
 F32 = mybir.dt.float32
 BF16 = mybir.dt.bfloat16
@@ -17,14 +18,23 @@ ACT = mybir.ActivationFunctionType
 ALU = mybir.AluOpType
 
 P = 128
+PIECES = J // P
 HALF = J // 2
-PIECES = 4
-WIDTH = 512
+BLOCKS = K // 32
 EXP_CAP = float(2 ** 62)
+U_SIDE, V_SIDE = 0, 1
+
+PE_ADDED = PIECES - 1
+TAIL_ORDER = (0, 1, 3, 2)
+FINAL_PIECE = TAIL_ORDER[-1]
+EARLY_PIECES = 2
+
+WB_AT, WA_AT, VA_AT = 0, 4 * N * 4, 4 * N * 4 + 2 * N
+STAGED_AT = WA_AT - 256
 
 
-def load_scale_rows(queue, plane, scales, quads):
-    for quad in quads:
+def load_scale_rows(queue, plane, scales, quadrants):
+    for quad in quadrants:
         queue.dma_start(
             out=plane[32 * quad : 32 * quad + 4, :].bitcast(I32),
             in_=scales[0, 4 * quad : 4 * quad + 4, :].bitcast(I32),
@@ -33,6 +43,10 @@ def load_scale_rows(queue, plane, scales, quads):
 
 def fp8_words(words):
     return words[0].rearrange("p n t -> p (n t)").bitcast(I32)
+
+
+def runs(ap, count):
+    return ap.rearrange("p (a c) -> p a c", a=count)
 
 
 def tile_list_precision_weighted_pair_kernel(
@@ -50,7 +64,7 @@ def tile_list_precision_weighted_pair_kernel(
         xt_s = keep.tile([P, T], U8, name="xt_s", align_bytes=64)
         sx_w = keep.tile([P, 2 * J], U8, name="sx_w", align_bytes=64)
         vb_w = keep.tile([P, N], U32, name="vb_w", align_bytes=64)
-        staged = shared.tile([16, 3, N], U8, name="staged", align_bytes=64, offset=7936)
+        staged = shared.tile([BLOCKS, 3, N], U8, name="staged", align_bytes=64, offset=STAGED_AT)
         planes = keep.tile([P, 3, N], U8, name="planes", align_bytes=64)
         sx_s, vb_s, va_s = planes[:, 0, :], planes[:, 1, :], planes[:, 2, :]
         wa_s = keep.tile([P, N], U8, name="wa_s", align_bytes=64)
@@ -60,9 +74,11 @@ def tile_list_precision_weighted_pair_kernel(
         xg_w = [keep.tile([P, HALF], U32, name="xg_w%d" % h, align_bytes=64) for h in range(2)]
         xg_s = keep.tile([P, J], U8, name="xg_s", align_bytes=64)
 
-        nc.vector.memset(xt_s[:].bitcast(I32), 0)
-        nc.vector.memset(planes[:].rearrange("p a n -> p (a n)").bitcast(I32), 0)
-        nc.gpsimd.memset(wa_s[:].bitcast(I32), 0)
+        staged_words = staged[:].rearrange("p a n -> p (a n)").bitcast(I32)
+        plane_words = planes[:].rearrange("p a n -> p (a n)").bitcast(I32)
+        nc.gpsimd.memset(xt_s[:].bitcast(I32), 0)
+        nc.vector.memset(plane_words, 0)
+        nc.vector.memset(wa_s[:].bitcast(I32), 0)
 
         for place, scales in enumerate((sx_scales, vb_scales, va_scales)):
             nc.sync.dma_start(out=staged[:, place, :].bitcast(I32), in_=scales[0].bitcast(I32))
@@ -70,143 +86,163 @@ def tile_list_precision_weighted_pair_kernel(
         nc.scalar.dma_start(out=vb_w[:].bitcast(I32), in_=fp8_words(vb_words))
         nc.sync.dma_start(offsets[:], offs)
         nc.sync.dma_start(out=xt_w[:].bitcast(I32), in_=fp8_words(xt_words))
-        load_scale_rows(nc.sync, xt_s, xt_scales, range(4))
-        staged_words = staged[:].rearrange("p a n -> p (a n)").bitcast(I32)
-        plane_words = planes[:].rearrange("p a n -> p (a n)").bitcast(I32)
+        load_scale_rows(nc.sync, xt_s, xt_scales, (0, 2))
+        load_scale_rows(nc.gpsimd, xt_s, xt_scales, (1, 3))
         nc.vector.tensor_copy(out=plane_words[0:4], in_=staged_words[0:4])
         for quad in range(1, 4):
             nc.sync.dma_start(
                 out=plane_words[32 * quad : 32 * quad + 4], in_=staged_words[4 * quad : 4 * quad + 4]
             )
-        wb_raw = shared.tile([P, 2, 4, N // 2], F32, name="wb_raw", align_bytes=64, offset=0)
-        wa_w = shared.tile([P, 2 * N], U8, name="wa_w", align_bytes=64, offset=8192)
-        va_w = shared.tile([P, N], U32, name="va_w", align_bytes=64, offset=9216)
+
+        wb_raw = shared.tile([P, 2, 4, N // 2], F32, name="wb_raw", align_bytes=64, offset=WB_AT)
+        wa_w = shared.tile([P, 2 * N], U8, name="wa_w", align_bytes=64, offset=WA_AT)
+        va_w = shared.tile([P, N], U32, name="va_w", align_bytes=64, offset=VA_AT)
+        wb_halves = [slice(half * (N // 2), (half + 1) * (N // 2)) for half in range(2)]
         nc.sync.dma_start(out=va_w[:].bitcast(I32), in_=fp8_words(va_words))
-        for half in range(2):
-            nc.sync.dma_start(
-                out=wb_raw[:, half],
-                in_=wb[:, half * (N // 2) : (half + 1) * (N // 2)].rearrange("(p t) n -> p t n", t=4),
-            )
+        for half, cols in enumerate(wb_halves):
+            nc.sync.dma_start(out=wb_raw[:, half], in_=wb[:, cols].rearrange("(p t) n -> p t n", t=4))
         nc.sync.dma_start(out=wa_w[:].bitcast(I32), in_=wa_words[0].bitcast(I32))
         load_scale_rows(nc.gpsimd, wa_s, wa_scales, range(4))
 
-        def product(bank, q, weights, weight_scales, moving, moving_scales):
-            h, pair = divmod(q, 2)
-            acc = psum.tile([P, WIDTH], F32, name="acc", tag="bank%d" % bank)
-            for s in range(2):
-                nt = 2 * pair + s
-                nc.tensor.matmul_mx(
-                    out=acc[:, s * HALF : (s + 1) * HALF],
-                    lhsT=weights(nt),
-                    lhsT_scale=weight_scales[:, nt * P : (nt + 1) * P],
-                    rhs=moving(h),
-                    rhs_scale=moving_scales[:, h * HALF : (h + 1) * HALF],
-                    start=True,
-                    stop=True,
-                )
+        identity = keep.tile([P, P], F32, name="identity")
+        make_identity(nc, identity[:])
+
+        def bank(index):
+            return psum.tile([P, N], F32, name="acc", tag="bank%d" % index)
+
+        def product(index, q, columns, column_scales, weights, weight_scales):
+            acc = bank(index)
+            nc.tensor.matmul_mx(
+                out=acc[:], lhsT=columns(q), lhsT_scale=column_scales[:, q * P : (q + 1) * P],
+                rhs=weights, rhs_scale=weight_scales, start=True, stop=True,
+            )
             return acc
 
-        def fp8_columns(words):
-            return lambda nt: words[:, nt * P : (nt + 1) * P].bitcast(FP8X4)
+        def turned_sum(index, addends):
+            acc = bank(index)
+            for place, addend in enumerate(addends):
+                for nt in range(4):
+                    nc.tensor.matmul(
+                        out=acc[:, nt * P : (nt + 1) * P], lhsT=addend[:, nt * P : (nt + 1) * P], rhs=identity[:],
+                        is_transpose=True, start=(place == 0 and nt == 0),
+                        stop=(place == len(addends) - 1 and nt == 3),
+                    )
+            return acc
 
-        def wa_columns(nt):
-            return wa_w[:, 2 * nt * P : 2 * (nt + 1) * P].bitcast(FP4X4)
+        def sx_columns(q):
+            return sx_w[:, 2 * q * P : 2 * (q + 1) * P].bitcast(FP4X4)
 
-        def sx_half(h):
-            return sx_w[:, 2 * h * HALF : 2 * (h + 1) * HALF].bitcast(FP4X4)
+        def xg_columns(q):
+            return xg_w[q // 2][:, (q % 2) * P : (q % 2 + 1) * P].bitcast(FP8X4)
 
-        def xg_half(h):
-            return xg_w[h][:].bitcast(FP8X4)
-
-        exp_u = keep.tile([P, PIECES, WIDTH], F32, name="exp_u")
-        capped_u = keep.tile([P, PIECES, WIDTH], F32, name="capped_u")
-        capped_v = keep.tile([P, PIECES, WIDTH], F32, name="capped_v")
-        prec = keep.tile([P, PIECES, 2, WIDTH], F32, name="prec")
-        late_terms = keep.tile([P, 2, 2, WIDTH], F32, name="late_terms")
-        den = keep.tile([P, PIECES, WIDTH], F32, name="den")
-        log_den = keep.tile([P, PIECES, WIDTH], F32, name="log_den")
-        num = keep.tile([P, PIECES, WIDTH], F32, name="num")
-        result = keep.tile([P, PIECES, WIDTH], F32, name="result")
-
-        def quarters(ap):
-            return ap.rearrange("p (a c) -> p a c", c=P)
-
-        def across(tile, q):
-            return tile[:, :, q * P : (q + 1) * P]
+        reused = keep.tile([P, 2 * PIECES, N], F32, name="reused")
+        capped_u = keep.tile([P, PIECES, N], F32, name="capped_u")
+        capped_v = keep.tile([P, PIECES, N], F32, name="capped_v")
+        prec = keep.tile([P, PIECES, 2, N], F32, name="prec")
+        late_terms = keep.tile([P, 2, PIECES - EARLY_PIECES, N], F32, name="late_terms")
+        den = keep.tile([P, PIECES - 1, N], F32, name="den")
+        log_den = keep.tile([P, PIECES, N + P], F32, name="log_den")
+        inverse = keep.tile([P, PIECES, N + P], F32, name="inverse")
+        num = keep.tile([P, PIECES - 1, N], F32, name="num")
+        result = keep.tile([P, PIECES, N], F32, name="result")
 
         def capped_exp(acc, grown, capped):
             nc.scalar.activation(out=grown, in_=acc[:], func=ACT.Exp)
             nc.vector.tensor_scalar(out=capped, in0=grown, scalar1=EXP_CAP, scalar2=None, op0=ALU.min)
 
-        v = [product(q, q, fp8_columns(vb_w), vb_s, sx_half, sx_s) for q in range(PIECES)]
+        v = [product(q, q, sx_columns, sx_s, vb_w[:].bitcast(FP8X4), vb_s) for q in range(PIECES)]
         for h in range(2):
             listed = offsets[:, h * (HALF // 16) : (h + 1) * (HALF // 16)]
             nc.vector.tensor_copy(xg_s[:, h * HALF : (h + 1) * HALF], xt_s[:].indirect(listed))
             nc.vector.tensor_copy(xg_w[h][:], xt_w[:].indirect(listed))
-        u = [product(PIECES + q, q, fp8_columns(va_w), va_s, xg_half, xg_s) for q in range(PIECES)]
+        u = [product(PIECES + q, q, xg_columns, xg_s, va_w[:].bitcast(FP8X4), va_s) for q in range(PIECES)]
         for q in range(PIECES):
             capped_exp(v[q], capped_v[:, q, :], capped_v[:, q, :])
         for q in range(PIECES):
-            capped_exp(u[q], exp_u[:, q, :], capped_u[:, q, :])
+            capped_exp(u[q], reused[:, q, :], capped_u[:, q, :])
 
-        for half in range(2):
-            cols = slice(half * (N // 2), (half + 1) * (N // 2))
+        for half, cols in enumerate(wb_halves):
             nc.vector.tensor_copy(
                 out=wb_bf[:, cols, :].rearrange("p (c i) t -> p c t i", i=4),
                 in_=wb_raw[:, half].rearrange("p t (c i) -> p c t i", i=4),
             )
-        for half in range(2):
-            cols = slice(half * (N // 2), (half + 1) * (N // 2))
+        for cols in wb_halves:
             nc.vector.quantize_mx(
                 out=wb_w[:, cols].bitcast(FP8X4),
                 scales=wb_s[:, cols],
                 in_=wb_bf[:, cols, :].rearrange("p n t -> p (n t)"),
             )
 
+        rows = 2 * PIECES
+
+        def logarithm(q, side):
+            first = (2 * q + 1 - side) * (N // rows)
+            return reused[:, :, first : first + N // rows]
+
         for q in range(PIECES):
-            nc.scalar.activation(out=across(exp_u, q), in_=quarters(capped_v[:, q, :]), func=ACT.Ln, bias=1.0)
-            nc.scalar.activation(out=capped_v[:, q, :], in_=capped_u[:, q, :], func=ACT.Ln, bias=1.0)
+            for side, capped in ((V_SIDE, capped_v), (U_SIDE, capped_u)):
+                nc.scalar.activation(out=logarithm(q, side), in_=runs(capped[:, q, :], rows), func=ACT.Ln, bias=1.0)
         for q in range(PIECES):
-            nc.vector.tensor_tensor(
-                out=quarters(prec[:, q, 1, :]), in0=quarters(v[q][:]), in1=across(exp_u, q), op=ALU.max
-            )
-            nc.vector.tensor_tensor(out=prec[:, q, 0, :], in0=u[q][:], in1=capped_v[:, q, :], op=ALU.max)
-            nc.gpsimd.tensor_tensor(out=den[:, q, :], in0=prec[:, q, 0, :], in1=prec[:, q, 1, :], op=ALU.add)
-        for q in range(PIECES):
-            nc.scalar.activation(out=log_den[:, q, :], in_=den[:, q, :], func=ACT.Ln, bias=0.1)
+            for side, acc in ((V_SIDE, v[q]), (U_SIDE, u[q])):
+                nc.vector.tensor_tensor(
+                    out=runs(prec[:, q, side, :], rows), in0=runs(acc[:], rows), in1=logarithm(q, side), op=ALU.max
+                )
+            if q != PE_ADDED:
+                nc.gpsimd.tensor_tensor(
+                    out=den[:, q, :], in0=prec[:, q, U_SIDE, :], in1=prec[:, q, V_SIDE, :], op=ALU.add
+                )
 
         def term(q, side):
-            return across(capped_v, 2 * q + side) if q < 2 else quarters(late_terms[:, q - 2, side, :])
+            if q < EARLY_PIECES:
+                row = 2 * (2 * q + side)
+                return reused[:, row : row + 2, N // 2 :]
+            return runs(late_terms[:, side, q - EARLY_PIECES, :], 2)
 
-        def add_terms(engine, q):
-            engine.tensor_tensor(out=quarters(num[:, q, :]), in0=term(q, 0), in1=term(q, 1), op=ALU.add)
+        def place_of(tile, q):
+            return runs(tile[:, q, :N], 4) if q != FINAL_PIECE else tile[:, :, N:]
+
+        def estimates(q):
+            b = product(q, q, sx_columns, sx_s, wb_w[:].bitcast(FP8X4), wb_s[:])
+            a = product(PIECES + q, q, xg_columns, xg_s, wa_w[:].bitcast(FP4X4), wa_s[:])
+            return a, b
+
+        den_bank = dict(zip(TAIL_ORDER, (2, PIECES + 2, 3, PIECES + 3)))
+        num_bank = (0, PIECES, 1, PIECES + 1)
+
+        early = [estimates(q) for q in range(EARLY_PIECES)]
+        for q in TAIL_ORDER:
+            addends = [den[:, q, :]] if q != PE_ADDED else [prec[:, q, V_SIDE, :], prec[:, q, U_SIDE, :]]
+            den_t = turned_sum(den_bank[q], addends)
+            nc.scalar.activation(out=place_of(log_den, q), in_=runs(den_t[:], 4), func=ACT.Ln, bias=0.1)
 
         for q in range(PIECES):
-            b = product(q, q, fp8_columns(wb_w), wb_s, sx_half, sx_s)
-            a = product(PIECES + q, q, wa_columns, wa_s, xg_half, xg_s)
-            nc.vector.tensor_tensor(out=term(q, 1), in0=quarters(b[:]), in1=quarters(prec[:, q, 1, :]), op=ALU.mult)
-            nc.vector.tensor_tensor(out=term(q, 0), in0=quarters(a[:]), in1=quarters(prec[:, q, 0, :]), op=ALU.mult)
-            if q < 2:
-                add_terms(nc.gpsimd, q)
-        for q in range(2, PIECES):
-            add_terms(nc.vector, q)
-
-        for q in range(PIECES):
-            nc.scalar.activation(out=across(den, q), in_=quarters(log_den[:, q, :]), func=ACT.Exp, scale=-1.0)
-        for q in range(PIECES):
-            h, pair = divmod(q, 2)
-            steps = 2 if q == PIECES - 1 else 1
-            for step in range(steps):
-                part = slice(step * 4 // steps, (step + 1) * 4 // steps)
-                tiles = slice(step * 2 // steps, (step + 1) * 2 // steps)
+            a, b = early[q] if q < EARLY_PIECES else estimates(q)
+            for side, acc in ((V_SIDE, b), (U_SIDE, a)):
                 nc.vector.tensor_tensor(
-                    out=quarters(result[:, q, :])[:, part],
-                    in0=quarters(num[:, q, :])[:, part],
-                    in1=across(den, q)[:, part],
-                    op=ALU.mult,
+                    out=term(q, side), in0=runs(acc[:], 2), in1=runs(prec[:, q, side, :], 2), op=ALU.mult
                 )
-                rows = out[2 * pair * P : 2 * (pair + 1) * P, h * HALF : (h + 1) * HALF]
+            if q != PE_ADDED:
+                nc.gpsimd.tensor_tensor(
+                    out=runs(num[:, q, :], 2), in0=term(q, U_SIDE), in1=term(q, V_SIDE), op=ALU.add
+                )
+        num_t = {}
+        for q in TAIL_ORDER:
+            if q != PE_ADDED:
+                addends = [num[:, q, :]]
+            else:
+                addends = [late_terms[:, side, q - EARLY_PIECES, :] for side in (V_SIDE, U_SIDE)]
+            num_t[q] = turned_sum(num_bank[q], addends)
+
+        for q in TAIL_ORDER:
+            cols = slice(0 if q != FINAL_PIECE else N, N + P)
+            nc.scalar.activation(out=inverse[:, q, cols], in_=log_den[:, q, cols], func=ACT.Exp, scale=-1.0)
+        for q in TAIL_ORDER:
+            for part in (slice(0, 2), slice(2, 4)) if q == FINAL_PIECE else (slice(0, 4),):
+                nc.vector.tensor_tensor(
+                    out=runs(result[:, q, :], 4)[:, part], in0=runs(num_t[q][:], 4)[:, part],
+                    in1=place_of(inverse, q)[:, part], op=ALU.mult,
+                )
                 nc.sync.dma_start(
-                    out=rows.rearrange("(s p) j -> p s j", p=P)[:, tiles],
-                    in_=result[:, q, :].rearrange("p (s j) -> p s j", s=2)[:, tiles],
+                    out=out[:, q * P : (q + 1) * P].rearrange("(nt p) j -> p nt j", p=P)[:, part],
+                    in_=runs(result[:, q, :], 4)[:, part],
                 )

from contextlib import ExitStack

import concourse.mybir as mybir
from concourse.masks import make_identity

K, T, J, N = 512, 2048, 512, 512
FLOPS = 4 * 2 * K * J * N

F32 = mybir.dt.float32
BF16 = mybir.dt.bfloat16
I32 = mybir.dt.int32
U32 = mybir.dt.uint32
U16 = mybir.dt.uint16
U8 = mybir.dt.uint8
FP8X4 = mybir.dt.float8_e4m3fn_x4
FP4X4 = mybir.dt.float4_e2m1fn_x4
ACT = mybir.ActivationFunctionType
ALU = mybir.AluOpType

P = 128
PIECES = J // P
HALF = J // 2
BLOCKS = K // 32
EXP_CAP = float(2 ** 62)
U_SIDE, V_SIDE = 0, 1

PE_ADDED = PIECES - 1
TAIL_ORDER = (0, 1, 3, 2)
FINAL_PIECE = TAIL_ORDER[-1]
EARLY_PIECES = 2

WB_AT, WA_AT, VA_AT = 0, 4 * N * 4, 4 * N * 4 + 2 * N
STAGED_AT = WA_AT - 256


def load_scale_rows(queue, plane, scales, quadrants):
    for quad in quadrants:
        queue.dma_start(
            out=plane[32 * quad : 32 * quad + 4, :].bitcast(I32),
            in_=scales[0, 4 * quad : 4 * quad + 4, :].bitcast(I32),
        )


def fp8_words(words):
    return words[0].rearrange("p n t -> p (n t)").bitcast(I32)


def runs(ap, count):
    return ap.rearrange("p (a c) -> p a c", a=count)


def tile_list_precision_weighted_pair_kernel(
    tc, xt_words, xt_scales, wa_words, wa_scales, va_words, va_scales,
    sx_words, sx_scales, wb, vb_words, vb_scales, offs, out,
):
    nc = tc.nc
    with ExitStack() as ctx:
        keep = ctx.enter_context(tc.tile_pool(name="keep", bufs=1))
        shared = ctx.enter_context(tc.tile_pool(name="shared", bufs=1))
        psum = ctx.enter_context(tc.psum_pool(name="psum", bufs=1))

        offsets = keep.tile([P, J // 16], U16, name="offsets")
        xt_w = keep.tile([P, T], U32, name="xt_w", align_bytes=64)
        xt_s = keep.tile([P, T], U8, name="xt_s", align_bytes=64)
        sx_w = keep.tile([P, 2 * J], U8, name="sx_w", align_bytes=64)
        vb_w = keep.tile([P, N], U32, name="vb_w", align_bytes=64)
        staged = shared.tile([BLOCKS, 3, N], U8, name="staged", align_bytes=64, offset=STAGED_AT)
        planes = keep.tile([P, 3, N], U8, name="planes", align_bytes=64)
        sx_s, vb_s, va_s = planes[:, 0, :], planes[:, 1, :], planes[:, 2, :]
        wa_s = keep.tile([P, N], U8, name="wa_s", align_bytes=64)
        wb_bf = keep.tile([P, N, 4], BF16, name="wb_bf", align_bytes=64)
        wb_w = keep.tile([P, N], U32, name="wb_w", align_bytes=64)
        wb_s = keep.tile([P, N], U8, name="wb_s", align_bytes=64)
        xg_w = [keep.tile([P, HALF], U32, name="xg_w%d" % h, align_bytes=64) for h in range(2)]
        xg_s = keep.tile([P, J], U8, name="xg_s", align_bytes=64)

        staged_words = staged[:].rearrange("p a n -> p (a n)").bitcast(I32)
        plane_words = planes[:].rearrange("p a n -> p (a n)").bitcast(I32)
        nc.gpsimd.memset(xt_s[:].bitcast(I32), 0)
        nc.vector.memset(plane_words, 0)
        nc.vector.memset(wa_s[:].bitcast(I32), 0)

        for place, scales in enumerate((sx_scales, vb_scales, va_scales)):
            nc.sync.dma_start(out=staged[:, place, :].bitcast(I32), in_=scales[0].bitcast(I32))
        nc.scalar.dma_start(out=sx_w[:].bitcast(I32), in_=sx_words[0].bitcast(I32))
        nc.scalar.dma_start(out=vb_w[:].bitcast(I32), in_=fp8_words(vb_words))
        nc.sync.dma_start(offsets[:], offs)
        nc.sync.dma_start(out=xt_w[:].bitcast(I32), in_=fp8_words(xt_words))
        load_scale_rows(nc.sync, xt_s, xt_scales, (0, 2))
        load_scale_rows(nc.gpsimd, xt_s, xt_scales, (1, 3))
        nc.vector.tensor_copy(out=plane_words[0:4], in_=staged_words[0:4])
        for quad in range(1, 4):
            nc.sync.dma_start(
                out=plane_words[32 * quad : 32 * quad + 4], in_=staged_words[4 * quad : 4 * quad + 4]
            )

        wb_raw = shared.tile([P, 2, 4, N // 2], F32, name="wb_raw", align_bytes=64, offset=WB_AT)
        wa_w = shared.tile([P, 2 * N], U8, name="wa_w", align_bytes=64, offset=WA_AT)
        va_w = shared.tile([P, N], U32, name="va_w", align_bytes=64, offset=VA_AT)
        wb_halves = [slice(half * (N // 2), (half + 1) * (N // 2)) for half in range(2)]
        nc.sync.dma_start(out=va_w[:].bitcast(I32), in_=fp8_words(va_words))
        for half, cols in enumerate(wb_halves):
            nc.sync.dma_start(out=wb_raw[:, half], in_=wb[:, cols].rearrange("(p t) n -> p t n", t=4))
        nc.sync.dma_start(out=wa_w[:].bitcast(I32), in_=wa_words[0].bitcast(I32))
        load_scale_rows(nc.gpsimd, wa_s, wa_scales, range(4))

        identity = keep.tile([P, P], F32, name="identity")
        make_identity(nc, identity[:])

        def bank(index):
            return psum.tile([P, N], F32, name="acc", tag="bank%d" % index)

        def product(index, q, columns, column_scales, weights, weight_scales):
            acc = bank(index)
            nc.tensor.matmul_mx(
                out=acc[:], lhsT=columns(q), lhsT_scale=column_scales[:, q * P : (q + 1) * P],
                rhs=weights, rhs_scale=weight_scales, start=True, stop=True,
            )
            return acc

        def turned_sum(index, addends):
            acc = bank(index)
            for place, addend in enumerate(addends):
                for nt in range(4):
                    nc.tensor.matmul(
                        out=acc[:, nt * P : (nt + 1) * P], lhsT=addend[:, nt * P : (nt + 1) * P], rhs=identity[:],
                        is_transpose=True, start=(place == 0 and nt == 0),
                        stop=(place == len(addends) - 1 and nt == 3),
                    )
            return acc

        def sx_columns(q):
            return sx_w[:, 2 * q * P : 2 * (q + 1) * P].bitcast(FP4X4)

        def xg_columns(q):
            return xg_w[q // 2][:, (q % 2) * P : (q % 2 + 1) * P].bitcast(FP8X4)

        reused = keep.tile([P, 2 * PIECES, N], F32, name="reused")
        capped_u = keep.tile([P, PIECES, N], F32, name="capped_u")
        capped_v = keep.tile([P, PIECES, N], F32, name="capped_v")
        prec = keep.tile([P, PIECES, 2, N], F32, name="prec")
        late_terms = keep.tile([P, 2, PIECES - EARLY_PIECES, N], F32, name="late_terms")
        den = keep.tile([P, PIECES - 1, N], F32, name="den")
        log_den = keep.tile([P, PIECES, N + P], F32, name="log_den")
        inverse = keep.tile([P, PIECES, N + P], F32, name="inverse")
        num = keep.tile([P, PIECES - 1, N], F32, name="num")
        result = keep.tile([P, PIECES, N], F32, name="result")

        def capped_exp(acc, grown, capped):
            nc.scalar.activation(out=grown, in_=acc[:], func=ACT.Exp)
            nc.vector.tensor_scalar(out=capped, in0=grown, scalar1=EXP_CAP, scalar2=None, op0=ALU.min)

        v = [product(q, q, sx_columns, sx_s, vb_w[:].bitcast(FP8X4), vb_s) for q in range(PIECES)]
        for h in range(2):
            listed = offsets[:, h * (HALF // 16) : (h + 1) * (HALF // 16)]
            nc.vector.tensor_copy(xg_s[:, h * HALF : (h + 1) * HALF], xt_s[:].indirect(listed))
            nc.vector.tensor_copy(xg_w[h][:], xt_w[:].indirect(listed))
        u = [product(PIECES + q, q, xg_columns, xg_s, va_w[:].bitcast(FP8X4), va_s) for q in range(PIECES)]
        for q in range(PIECES):
            capped_exp(v[q], capped_v[:, q, :], capped_v[:, q, :])
        for q in range(PIECES):
            capped_exp(u[q], reused[:, q, :], capped_u[:, q, :])

        for half, cols in enumerate(wb_halves):
            nc.vector.tensor_copy(
                out=wb_bf[:, cols, :].rearrange("p (c i) t -> p c t i", i=4),
                in_=wb_raw[:, half].rearrange("p t (c i) -> p c t i", i=4),
            )
        for cols in wb_halves:
            nc.vector.quantize_mx(
                out=wb_w[:, cols].bitcast(FP8X4),
                scales=wb_s[:, cols],
                in_=wb_bf[:, cols, :].rearrange("p n t -> p (n t)"),
            )

        rows = 2 * PIECES

        def logarithm(q, side):
            first = (2 * q + 1 - side) * (N // rows)
            return reused[:, :, first : first + N // rows]

        for q in range(PIECES):
            for side, capped in ((V_SIDE, capped_v), (U_SIDE, capped_u)):
                nc.scalar.activation(out=logarithm(q, side), in_=runs(capped[:, q, :], rows), func=ACT.Ln, bias=1.0)
        for q in range(PIECES):
            for side, acc in ((V_SIDE, v[q]), (U_SIDE, u[q])):
                nc.vector.tensor_tensor(
                    out=runs(prec[:, q, side, :], rows), in0=runs(acc[:], rows), in1=logarithm(q, side), op=ALU.max
                )
            if q != PE_ADDED:
                nc.gpsimd.tensor_tensor(
                    out=den[:, q, :], in0=prec[:, q, U_SIDE, :], in1=prec[:, q, V_SIDE, :], op=ALU.add
                )

        def term(q, side):
            if q < EARLY_PIECES:
                row = 2 * (2 * q + side)
                return reused[:, row : row + 2, N // 2 :]
            return runs(late_terms[:, side, q - EARLY_PIECES, :], 2)

        def place_of(tile, q):
            return runs(tile[:, q, :N], 4) if q != FINAL_PIECE else tile[:, :, N:]

        def estimates(q):
            b = product(q, q, sx_columns, sx_s, wb_w[:].bitcast(FP8X4), wb_s[:])
            a = product(PIECES + q, q, xg_columns, xg_s, wa_w[:].bitcast(FP4X4), wa_s[:])
            return a, b

        den_bank = dict(zip(TAIL_ORDER, (2, PIECES + 2, 3, PIECES + 3)))
        num_bank = (0, PIECES, 1, PIECES + 1)

        early = [estimates(q) for q in range(EARLY_PIECES)]
        for q in TAIL_ORDER:
            addends = [den[:, q, :]] if q != PE_ADDED else [prec[:, q, V_SIDE, :], prec[:, q, U_SIDE, :]]
            den_t = turned_sum(den_bank[q], addends)
            nc.scalar.activation(out=place_of(log_den, q), in_=runs(den_t[:], 4), func=ACT.Ln, bias=0.1)

        for q in range(PIECES):
            a, b = early[q] if q < EARLY_PIECES else estimates(q)
            for side, acc in ((V_SIDE, b), (U_SIDE, a)):
                nc.vector.tensor_tensor(
                    out=term(q, side), in0=runs(acc[:], 2), in1=runs(prec[:, q, side, :], 2), op=ALU.mult
                )
            if q != PE_ADDED:
                nc.gpsimd.tensor_tensor(
                    out=runs(num[:, q, :], 2), in0=term(q, U_SIDE), in1=term(q, V_SIDE), op=ALU.add
                )
        num_t = {}
        for q in TAIL_ORDER:
            if q != PE_ADDED:
                addends = [num[:, q, :]]
            else:
                addends = [late_terms[:, side, q - EARLY_PIECES, :] for side in (V_SIDE, U_SIDE)]
            num_t[q] = turned_sum(num_bank[q], addends)

        for q in TAIL_ORDER:
            cols = slice(0 if q != FINAL_PIECE else N, N + P)
            nc.scalar.activation(out=inverse[:, q, cols], in_=log_den[:, q, cols], func=ACT.Exp, scale=-1.0)
        for q in TAIL_ORDER:
            for part in (slice(0, 2), slice(2, 4)) if q == FINAL_PIECE else (slice(0, 4),):
                nc.vector.tensor_tensor(
                    out=runs(result[:, q, :], 4)[:, part], in0=runs(num_t[q][:], 4)[:, part],
                    in1=place_of(inverse, q)[:, part], op=ALU.mult,
                )
                nc.sync.dma_start(
                    out=out[:, q * P : (q + 1) * P].rearrange("(nt p) j -> p nt j", p=P)[:, part],
                    in_=runs(result[:, q, :], 4)[:, part],
                )
